import numpy as np
CORES = [66,70,74,78,82,86,90,94,98,102,106,110,114,118,122,126]
N = 16
TK = 256
D = 128 * N
EPS = 0.01
def setup_inputs(rng):
    return {"x": (rng.standard_normal((N, 128, TK), dtype=np.float32) * (0.5 + np.abs(rng.standard_normal((1, 1, TK), dtype=np.float32))) + rng.standard_normal((1, 1, TK), dtype=np.float32))}
def setup_inputs_big(rng):
    d = setup_inputs(rng)
    for k in ("x",): d[k] = (d[k].astype(np.float32) * 1024.0).astype(d[k].dtype)
    return d
def setup_inputs_small(rng):
    d = setup_inputs(rng)
    for k in ("x",): d[k] = (d[k].astype(np.float32) * (1 / 1024.0)).astype(d[k].dtype)
    return d
def setup_inputs_apart(rng):
    d = setup_inputs(rng)
    f = (10.0 ** rng.permutation(np.linspace(-1.5, 1.5, N))).astype(np.float32).reshape(N, 1, 1)
    for k in ("x",): d[k] = (d[k].astype(np.float32) * f).astype(d[k].dtype)
    return d
def setup_inputs_mixed(rng):
    d = setup_inputs(rng)
    f = (10.0 ** rng.uniform(-3, 3, (1, 1, TK))).astype(np.float32); shape = rng.integers(3, size=(1, 1, TK))
    for k in ("x",):
        x = d[k].astype(np.float32)
        m = x.mean(axis=(0, 1), keepdims=True); level = m + np.sign(x - m) * np.abs(x - m).mean(axis=(0, 1), keepdims=True) * rng.uniform(0.9, 1.1, x.shape).astype(np.float32)
        other = x * np.where(rng.random(x.shape) < 0.5, 0.1, 1.0).astype(np.float32)
        d[k] = (np.where(shape == 1, level, np.where(shape == 2, other, x)) * f).astype(d[k].dtype)
    return d
def setup_inputs_offset(rng):
    d = setup_inputs(rng)
    x = d["x"]; spread = x.std(axis=(0, 1), keepdims=True)
    d["x"] = (x + spread * rng.uniform(16, 48, (1, 1, TK)) * rng.choice([-1.0, 1.0], (1, 1, TK))).astype(np.float32)
    return d
def reference(x):
    X = x.astype(np.float64)
    mu = X.sum(axis=(0, 1)) / D
    Z = X - mu
    Z = Z / np.sqrt((Z ** 2).sum(axis=(0, 1)) / D + EPS)
    return {"y": Z.astype(np.float32)}

@@ -1,0 +1,169 @@
+import math
+from concourse.bass import DstId, RemoteDMATransfer
+from concourse.mybir import AluOpType, AxisListType, ActivationFunctionType
+
+NR = 16
+DF = 2048
+EPS = 0.01
+
+SCRATCH = {
+    "xs": ("sbuf", [128, 256], "float32"),
+    "idn": ("sbuf", [128, 128], "float32"),
+    "onec": ("sbuf", [128, 1], "float32"),
+    "st": ("sbuf", [128, 4], "float32"),
+    "sums": ("sbuf", [128, 2], "float32"),
+    "negm": ("sbuf", [128, 2], "float32"),
+    "junk": ("sbuf", [128, 288], "float32"),
+    "dl": ("dram", [NR, 128, 4], "float32"),
+    "rk": ("sbuf", [128, 512], "float32"),
+    "negu": ("sbuf", [128, 2], "float32"),
+    "mu": ("sbuf", [128, 2], "float32"),
+    "qe": ("sbuf", [128, 2], "float32"),
+    "e2": ("sbuf", [128, 2], "float32"),
+    "var": ("sbuf", [128, 2], "float32"),
+    "sdv": ("sbuf", [128, 2], "float32"),
+    "r0": ("sbuf", [128, 2], "float32"),
+    "n1": ("sbuf", [128, 2], "float32"),
+    "n2": ("sbuf", [128, 2], "float32"),
+    "n3": ("sbuf", [128, 2], "float32"),
+    "zc": ("sbuf", [128, 256], "float32"),
+    "yt": ("sbuf", [128, 256], "float32"),
+    "ys": ("sbuf", [128, 256], "float32"),
+    "pt0": ("psum", [128, 512], "float32"),
+    "pt1": ("psum", [128, 512], "float32"),
+    "py0": ("psum", [128, 512], "float32"),
+    "py1": ("psum", [128, 512], "float32"),
+    "pu0": ("psum", [128, 512], "float32"),
+    "pu1": ("psum", [128, 512], "float32"),
+    "pq": ("psum", [128, 512], "float32"),
+}
+SEMAPHORES = ["ld", "m1", "m2", "ide", "t0", "t1", "a0", "a1", "b0", "b1", "u0", "u1", "q0", "q1", "sd", "arr", "loc",
+              "rdy", "pu0e", "pu1e", "pqe", "g0", "g1", "mue", "qee", "e0", "e1", "ve", "z0", "z1", "sqe", "rce",
+              "n1e", "n2e", "n3e", "y0", "y1", "py0e", "py1e", "c0", "c1", "s0", "s1"]
+
+
+def rank_program(g, core, T, topo):
+    rank = T.rank_of(core)
+    if rank is None:
+        return
+    S = T.sem
+    A = AluOpType
+    F = ActivationFunctionType
+    X = AxisListType.X
+    V, AC, PE, SY = g.vector, g.scalar, g.tensor, g.sync
+    cs = 1.0 / math.sqrt(float(DF))
+    pt = [T.pt0, T.pt1]
+    py = [T.py0, T.py1]
+    pu = [T.pu0, T.pu1]
+    H = [slice(0, 128), slice(128, 256)]
+    C = [slice(0, 1), slice(1, 2)]
+
+    SY.dma_start(T.xs[:], T.x[:]).then_inc(S.ld, 16)
+    V.memset(T.idn[:], 1.0).then_inc(S.m1, 1)
+    V.memset(T.onec[:], 1.0).then_inc(S.m2, 1)
+    g.wait_ge(S.m1, 1)
+    g.affine_select(T.idn[:], T.idn[:], [[-1, 128]], A.is_equal, 0.0, 0, 1).then_inc(S.ide, 1)
+    PE.wait_ge(S.ide, 1)
+    PE.wait_ge(S.m2, 1)
+    PE.wait_ge(S.ld, 16)
+    PE.transpose(pt[0][:, 0:128], T.xs[:, H[0]], T.idn[:]).then_inc(S.t0, 1)
+    PE.transpose(pt[1][:, 0:128], T.xs[:, H[1]], T.idn[:]).then_inc(S.t1, 1)
+
+    for h in (0, 1):
+        V.wait_ge(S["t%d" % h], 1)
+        V.tensor_reduce(T.sums[:, C[h]], pt[h][:, 0:128], X, A.add).then_inc(S["a%d" % h], 1)
+        V.wait_ge(S["a%d" % h], 1)
+        V.tensor_scalar(T.negm[:, C[h]], T.sums[:, C[h]], -cs / 128.0, None, A.mult).then_inc(S["b%d" % h], 1)
+        V.tensor_scalar(T.st[:, C[h]], T.sums[:, C[h]], 1.0 / 8192.0, None, A.mult).then_inc(S["u%d" % h], 1)
+        AC.wait_ge(S["b%d" % h], 1)
+        AC.activation(T.junk[:, H[h]], pt[h][:, 0:128], F.Square, bias=T.negm[:, C[h]], scale=cs,
+                      accum_out=T.st[:, 2 + h:3 + h]).then_inc(S["q%d" % h], 1)
+
+    for nm in ("u0", "u1", "q0", "q1"):
+        SY.wait_ge(S[nm], 1)
+    SY.dma_start(T.dl[rank], T.st[:]).then_inc(S.sd, 16)
+
+    def far(d):
+        a, b = topo.chip(core), topo.chip(d)
+        if a == b:
+            return 0
+        return 1 if (topo.mates(a, b) or topo.same_plane(a, b)) else 2
+
+    others = sorted([d for d in T.cores if d != core and topo.may_write(core, d)], key=lambda d: -far(d))
+    common = 0xFFFF
+    for d in others:
+        common &= topo.mask(core, d)
+    engines = [1 << i for i in range(16) if (common >> i) & 1]
+    transfers = []
+    for i, e in enumerate(engines):
+        ds = others[i::len(engines)]
+        if not ds:
+            continue
+        ids = []
+        for d in ds:
+            rid, pid, _ = topo.addr(d)
+            ids.append(DstId(rid=rid, pnc=pid))
+        transfers.append(RemoteDMATransfer(dst_ids=ids, dma_engine_mask=e, remote_sem=S.arr,
+                                           srcs=[T.dl[rank]], dsts=[T.dl[rank] for _ in ds], alu_op=0))
+    g.wait_ge(S.sd, 16)
+    g.remote_dma_fused(transfers, local_sem=S.loc)
+
+    SY.wait_ge(S.sd, 16)
+    SY.wait_ge(S.arr, len(others))
+    SY.dma_start(T.rk[0:NR, :], T.dl[:]).then_inc(S.rdy, 16)
+    PE.wait_ge(S.rdy, 16)
+    for h in (0, 1):
+        PE.matmul(pu[h][:, 0:NR], T.rk[0:NR, h:512:4], T.idn[0:NR, 0:NR], True, True).then_inc(S["pu%de" % h], 1)
+    for h in (0, 1):
+        PE.matmul(T.pq[:, C[h]], T.rk[0:NR, 2 + h:512:4], T.onec[0:NR, :], True, True).then_inc(S.pqe, 1)
+
+    for h in (0, 1):
+        V.wait_ge(S["pu%de" % h], 1)
+        V.tensor_reduce(T.negu[:, C[h]], pu[h][:, 0:NR], X, A.add, negate=True).then_inc(S["g%d" % h], 1)
+        AC.wait_ge(S["g%d" % h], 1)
+        AC.activation(T.junk[:, 256 + 16 * h:272 + 16 * h], pu[h][:, 0:NR], F.Square, bias=T.negu[:, C[h]],
+                      scale=16.0, accum_out=T.e2[:, C[h]]).then_inc(S["e%d" % h], 1)
+    V.wait_ge(S.g0, 1)
+    V.wait_ge(S.g1, 1)
+    V.tensor_scalar(T.mu[:], T.negu[:], -4.0, None, A.mult).then_inc(S.mue, 1)
+    V.wait_ge(S.pqe, 2)
+    V.tensor_scalar(T.qe[:], T.pq[:, 0:2], EPS, None, A.add).then_inc(S.qee, 1)
+    V.wait_ge(S.qee, 1)
+    V.wait_ge(S.e0, 1)
+    V.wait_ge(S.e1, 1)
+    V.tensor_tensor(T.var[:], T.e2[:], T.qe[:], A.add).then_inc(S.ve, 1)
+    AC.wait_ge(S.ve, 1)
+    AC.activation(T.sdv[:], T.var[:], F.Sqrt).then_inc(S.sqe, 1)
+    V.wait_ge(S.mue, 1)
+    for h in (0, 1):
+        V.wait_ge(S["q%d" % h], 1)
+        V.tensor_scalar(T.zc[:, H[h]], pt[h][:, 0:128], T.mu[:, C[h]], None, A.subtract).then_inc(S["z%d" % h], 1)
+    V.wait_ge(S.sqe, 1)
+    V.reciprocal(T.r0[:], T.sdv[:]).then_inc(S.rce, 1)
+    V.wait_ge(S.rce, 1)
+    V.wait_ge(S.ve, 1)
+    V.tensor_tensor(T.n1[:], T.var[:], T.r0[:], A.mult).then_inc(S.n1e, 1)
+    V.wait_ge(S.n1e, 1)
+    V.tensor_tensor(T.n2[:], T.n1[:], T.r0[:], A.mult).then_inc(S.n2e, 1)
+    V.wait_ge(S.n2e, 1)
+    V.tensor_scalar(T.n3[:], T.n2[:], -0.5, 1.5, A.mult, A.add).then_inc(S.n3e, 1)
+    V.wait_ge(S.n3e, 1)
+    for h in (0, 1):
+        V.wait_ge(S["z%d" % h], 1)
+        V.tensor_scalar(T.yt[:, H[h]], T.zc[:, H[h]], T.r0[:, C[h]], T.n3[:, C[h]], A.mult, A.mult).then_inc(
+            S["y%d" % h], 1)
+        PE.wait_ge(S["y%d" % h], 1)
+        PE.transpose(py[h][:, 0:128], T.yt[:, H[h]], T.idn[:]).then_inc(S["py%de" % h], 1)
+
+    AC.wait_ge(S.py0e, 1)
+    AC.activation(T.ys[:, H[0]], py[0][:, 0:128], F.Copy).then_inc(S.c0, 1)
+    AC.wait_ge(S.c0, 1)
+    AC.dma_start(T.y[:, H[0]], T.ys[:, H[0]]).then_inc(S.s0, 16)
+    V.wait_ge(S.py1e, 1)
+    V.tensor_copy(T.ys[:, H[1]], py[1][:, 0:128]).then_inc(S.c1, 1)
+    SY.wait_ge(S.c1, 1)
+    SY.dma_start(T.y[:, H[1]], T.ys[:, H[1]]).then_inc(S.s1, 16)
+
+    g.wait_ge(S.loc, len(transfers))
+    AC.wait_ge(S.s0, 16)
+    SY.wait_ge(S.s1, 16)

@@ -89,27 +89,40 @@ def rank_program(g, core, T, topo):
             return 0
         return 1 if (topo.mates(a, b) or topo.same_plane(a, b)) else 2
 
-    others = sorted([d for d in T.cores if d != core and topo.may_write(core, d)], key=lambda d: -far(d))
+    def ids_of(ds):
+        out = []
+        for d in ds:
+            rid, pid, _ = topo.addr(d)
+            out.append(DstId(rid=rid, pnc=pid))
+        return out
+
+    others = [d for d in T.cores if d != core and topo.may_write(core, d)]
+    here = [d for d in others if far(d) == 0]
+    away = sorted([d for d in others if far(d) > 0], key=lambda d: -far(d))
     common = 0xFFFF
     for d in others:
         common &= topo.mask(core, d)
     engines = [1 << i for i in range(16) if (common >> i) & 1]
+    left = 0
+    for nm in ("u0", "u1", "q0", "q1"):
+        g.wait_ge(S[nm], 1)
+    if here:
+        g.remote_dma_fused([RemoteDMATransfer(dst_ids=ids_of(here), dma_engine_mask=common, remote_sem=S.arr,
+                                              srcs=[T.st[:]], dsts=[T.dl[rank] for _ in here], alu_op=0)],
+                           local_sem=S.loc)
+        left += len(engines)
     transfers = []
     for i, e in enumerate(engines):
-        ds = others[i::len(engines)]
-        if not ds:
-            continue
-        ids = []
-        for d in ds:
-            rid, pid, _ = topo.addr(d)
-            ids.append(DstId(rid=rid, pnc=pid))
-        transfers.append(RemoteDMATransfer(dst_ids=ids, dma_engine_mask=e, remote_sem=S.arr,
-                                           srcs=[T.dl[rank]], dsts=[T.dl[rank] for _ in ds], alu_op=0))
+        ds = away[i::len(engines)]
+        if ds:
+            transfers.append(RemoteDMATransfer(dst_ids=ids_of(ds), dma_engine_mask=e, remote_sem=S.arr,
+                                               srcs=[T.dl[rank]], dsts=[T.dl[rank] for _ in ds], alu_op=0))
     g.wait_ge(S.sd, 16)
     g.remote_dma_fused(transfers, local_sem=S.loc)
+    left += len(transfers)
 
     SY.wait_ge(S.sd, 16)
-    SY.wait_ge(S.arr, len(others))
+    SY.wait_ge(S.arr, len(here) * len(engines) + len(away))
     SY.dma_start(T.rk[0:NR, :], T.dl[:]).then_inc(S.rdy, 16)
     PE.wait_ge(S.rdy, 16)
     for h in (0, 1):
@@ -164,6 +177,6 @@ def rank_program(g, core, T, topo):
     SY.wait_ge(S.c1, 1)
     SY.dma_start(T.y[:, H[1]], T.ys[:, H[1]]).then_inc(S.s1, 16)
 
-    g.wait_ge(S.loc, len(transfers))
+    g.wait_ge(S.loc, left)
     AC.wait_ge(S.s0, 16)
     SY.wait_ge(S.s1, 16)

@@ -16,16 +16,16 @@ SCRATCH = {
     "junk": ("sbuf", [128, 288], "float32"),
     "dl": ("dram", [NR, 128, 4], "float32"),
     "rk": ("sbuf", [128, 512], "float32"),
+    "sdo": ("sbuf", [128, 2], "float32"),
+    "av": ("sbuf", [128, 2], "float32"),
+    "a2": ("sbuf", [128, 2], "float32"),
     "negu": ("sbuf", [128, 2], "float32"),
     "mu": ("sbuf", [128, 2], "float32"),
     "qe": ("sbuf", [128, 2], "float32"),
     "e2": ("sbuf", [128, 2], "float32"),
-    "var": ("sbuf", [128, 2], "float32"),
+    "w": ("sbuf", [128, 2], "float32"),
     "sdv": ("sbuf", [128, 2], "float32"),
-    "r0": ("sbuf", [128, 2], "float32"),
-    "n1": ("sbuf", [128, 2], "float32"),
-    "n2": ("sbuf", [128, 2], "float32"),
-    "n3": ("sbuf", [128, 2], "float32"),
+    "rr": ("sbuf", [128, 2], "float32"),
     "zc": ("sbuf", [128, 256], "float32"),
     "yt": ("sbuf", [128, 256], "float32"),
     "ys": ("sbuf", [128, 256], "float32"),
@@ -38,8 +38,8 @@ SCRATCH = {
     "pq": ("psum", [128, 512], "float32"),
 }
 SEMAPHORES = ["ld", "m1", "m2", "ide", "t0", "t1", "a0", "a1", "b0", "b1", "u0", "u1", "q0", "q1", "sd", "arr", "loc",
-              "rdy", "pu0e", "pu1e", "pqe", "g0", "g1", "mue", "qee", "e0", "e1", "ve", "z0", "z1", "sqe", "rce",
-              "n1e", "n2e", "n3e", "y0", "y1", "py0e", "py1e", "c0", "c1", "s0", "s1"]
+              "rdy", "pu0e", "pu1e", "pqe", "g0", "g1", "mue", "qee", "e0", "e1", "w0", "w1", "z0", "z1", "sqe", "rce",
+              "soe", "ae", "a2e", "y0", "y1", "py0e", "py1e", "c0", "c1", "s0", "s1"]
 
 
 def rank_program(g, core, T, topo):
@@ -82,6 +82,14 @@ def rank_program(g, core, T, topo):
     for nm in ("u0", "u1", "q0", "q1"):
         SY.wait_ge(S[nm], 1)
     SY.dma_start(T.dl[rank], T.st[:]).then_inc(S.sd, 16)
+
+    AC.wait_ge(S.q0, 1)
+    AC.wait_ge(S.q1, 1)
+    AC.activation(T.sdo[:], T.st[:, 2:4], F.Sqrt, bias=EPS).then_inc(S.soe, 1)
+    V.wait_ge(S.soe, 1)
+    V.reciprocal(T.av[:], T.sdo[:]).then_inc(S.ae, 1)
+    V.wait_ge(S.ae, 1)
+    V.tensor_tensor(T.a2[:], T.av[:], T.av[:], A.mult).then_inc(S.a2e, 1)
 
     def far(d):
         a, b = topo.chip(core), topo.chip(d)
@@ -139,32 +147,28 @@ def rank_program(g, core, T, topo):
     V.wait_ge(S.g0, 1)
     V.wait_ge(S.g1, 1)
     V.tensor_scalar(T.mu[:], T.negu[:], -4.0, None, A.mult).then_inc(S.mue, 1)
+    V.wait_ge(S.mue, 1)
+    V.wait_ge(S.a2e, 1)
+    for h in (0, 1):
+        V.wait_ge(S["q%d" % h], 1)
+        V.tensor_scalar(T.zc[:, H[h]], pt[h][:, 0:128], T.mu[:, C[h]], T.av[:, C[h]], A.subtract, A.mult).then_inc(
+            S["z%d" % h], 1)
     V.wait_ge(S.pqe, 2)
     V.tensor_scalar(T.qe[:], T.pq[:, 0:2], EPS, None, A.add).then_inc(S.qee, 1)
     V.wait_ge(S.qee, 1)
-    V.wait_ge(S.e0, 1)
-    V.wait_ge(S.e1, 1)
-    V.tensor_tensor(T.var[:], T.e2[:], T.qe[:], A.add).then_inc(S.ve, 1)
-    AC.wait_ge(S.ve, 1)
-    AC.activation(T.sdv[:], T.var[:], F.Sqrt).then_inc(S.sqe, 1)
-    V.wait_ge(S.mue, 1)
     for h in (0, 1):
-        V.wait_ge(S["q%d" % h], 1)
-        V.tensor_scalar(T.zc[:, H[h]], pt[h][:, 0:128], T.mu[:, C[h]], None, A.subtract).then_inc(S["z%d" % h], 1)
+        V.wait_ge(S["e%d" % h], 1)
+        V.tensor_scalar(T.w[:, C[h]], T.e2[:, C[h]], T.qe[:, C[h]], T.a2[:, C[h]], A.add, A.mult).then_inc(
+            S["w%d" % h], 1)
+    AC.wait_ge(S.w0, 1)
+    AC.wait_ge(S.w1, 1)
+    AC.activation(T.sdv[:], T.w[:], F.Sqrt).then_inc(S.sqe, 1)
     V.wait_ge(S.sqe, 1)
-    V.reciprocal(T.r0[:], T.sdv[:]).then_inc(S.rce, 1)
+    V.reciprocal(T.rr[:], T.sdv[:]).then_inc(S.rce, 1)
     V.wait_ge(S.rce, 1)
-    V.wait_ge(S.ve, 1)
-    V.tensor_tensor(T.n1[:], T.var[:], T.r0[:], A.mult).then_inc(S.n1e, 1)
-    V.wait_ge(S.n1e, 1)
-    V.tensor_tensor(T.n2[:], T.n1[:], T.r0[:], A.mult).then_inc(S.n2e, 1)
-    V.wait_ge(S.n2e, 1)
-    V.tensor_scalar(T.n3[:], T.n2[:], -0.5, 1.5, A.mult, A.add).then_inc(S.n3e, 1)
-    V.wait_ge(S.n3e, 1)
     for h in (0, 1):
         V.wait_ge(S["z%d" % h], 1)
-        V.tensor_scalar(T.yt[:, H[h]], T.zc[:, H[h]], T.r0[:, C[h]], T.n3[:, C[h]], A.mult, A.mult).then_inc(
-            S["y%d" % h], 1)
+        V.tensor_scalar(T.yt[:, H[h]], T.zc[:, H[h]], T.rr[:, C[h]], None, A.mult).then_inc(S["y%d" % h], 1)
         PE.wait_ge(S["y%d" % h], 1)
         PE.transpose(py[h][:, 0:128], T.yt[:, H[h]], T.idn[:]).then_inc(S["py%de" % h], 1)
 

@@ -1,34 +1,30 @@
-import math
 from concourse.bass import DstId, RemoteDMATransfer
-from concourse.mybir import AluOpType, AxisListType, ActivationFunctionType
+from concourse.mybir import AluOpType, ActivationFunctionType
 
 NR = 16
-DF = 2048
 EPS = 0.01
 
 SCRATCH = {
     "xs": ("sbuf", [128, 256], "float32"),
     "idn": ("sbuf", [128, 128], "float32"),
-    "onec": ("sbuf", [128, 1], "float32"),
+    "nc": ("sbuf", [128, 1], "float32"),
+    "hc": ("sbuf", [128, 1], "float32"),
+    "wm": ("sbuf", [128, 20], "float32"),
     "st": ("sbuf", [128, 4], "float32"),
-    "sums": ("sbuf", [128, 2], "float32"),
-    "negm": ("sbuf", [128, 2], "float32"),
     "junk": ("sbuf", [128, 288], "float32"),
     "dl": ("dram", [NR, 128, 4], "float32"),
     "rk": ("sbuf", [128, 512], "float32"),
     "sdo": ("sbuf", [128, 2], "float32"),
     "av": ("sbuf", [128, 2], "float32"),
     "a2": ("sbuf", [128, 2], "float32"),
-    "negu": ("sbuf", [128, 2], "float32"),
-    "mu": ("sbuf", [128, 2], "float32"),
-    "qe": ("sbuf", [128, 2], "float32"),
     "e2": ("sbuf", [128, 2], "float32"),
-    "w": ("sbuf", [128, 2], "float32"),
+    "bb": ("sbuf", [128, 2], "float32"),
     "sdv": ("sbuf", [128, 2], "float32"),
     "rr": ("sbuf", [128, 2], "float32"),
     "zc": ("sbuf", [128, 256], "float32"),
     "yt": ("sbuf", [128, 256], "float32"),
     "ys": ("sbuf", [128, 256], "float32"),
+    "pm": ("psum", [128, 512], "float32"),
     "pt0": ("psum", [128, 512], "float32"),
     "pt1": ("psum", [128, 512], "float32"),
     "py0": ("psum", [128, 512], "float32"),
@@ -37,9 +33,9 @@ SCRATCH = {
     "pu1": ("psum", [128, 512], "float32"),
     "pq": ("psum", [128, 512], "float32"),
 }
-SEMAPHORES = ["ld", "m1", "m2", "ide", "t0", "t1", "a0", "a1", "b0", "b1", "u0", "u1", "q0", "q1", "sd", "arr", "loc",
-              "rdy", "pu0e", "pu1e", "pqe", "g0", "g1", "mue", "qee", "e0", "e1", "w0", "w1", "z0", "z1", "sqe", "rce",
-              "soe", "ae", "a2e", "y0", "y1", "py0e", "py1e", "c0", "c1", "s0", "s1"]
+SEMAPHORES = ["ld", "m1", "wk", "ide", "nn", "t0", "t1", "ue", "q0", "q1", "sd", "arr", "loc", "rdy", "pu0e", "pu1e",
+              "pqe", "e0", "e1", "w0", "w1", "z0", "z1", "sq", "rc", "soe", "ae", "a2e", "y0", "y1", "py0e", "py1e",
+              "c0", "c1", "s0", "s1"]
 
 
 def rank_program(g, core, T, topo):
@@ -49,9 +45,7 @@ def rank_program(g, core, T, topo):
     S = T.sem
     A = AluOpType
     F = ActivationFunctionType
-    X = AxisListType.X
     V, AC, PE, SY = g.vector, g.scalar, g.tensor, g.sync
-    cs = 1.0 / math.sqrt(float(DF))
     pt = [T.pt0, T.pt1]
     py = [T.py0, T.py1]
     pu = [T.pu0, T.pu1]
@@ -60,32 +54,36 @@ def rank_program(g, core, T, topo):
 
     SY.dma_start(T.xs[:], T.x[:]).then_inc(S.ld, 16)
     V.memset(T.idn[:], 1.0).then_inc(S.m1, 1)
-    V.memset(T.onec[:], 1.0).then_inc(S.m2, 1)
     g.wait_ge(S.m1, 1)
     g.affine_select(T.idn[:], T.idn[:], [[-1, 128]], A.is_equal, 0.0, 0, 1).then_inc(S.ide, 1)
-    PE.wait_ge(S.ide, 1)
-    PE.wait_ge(S.m2, 1)
-    PE.wait_ge(S.ld, 16)
-    PE.transpose(pt[0][:, 0:128], T.xs[:, H[0]], T.idn[:]).then_inc(S.t0, 1)
-    PE.transpose(pt[1][:, 0:128], T.xs[:, H[1]], T.idn[:]).then_inc(S.t1, 1)
+    V.memset(T.nc[:], -1.0 / 4096.0).then_inc(S.wk, 1)
+    V.memset(T.hc[:], 0.5).then_inc(S.wk, 1)
+    V.memset(T.wm[0:NR, NR:NR + 1], -2.0).then_inc(S.wk, 1)
+    V.wait_ge(S.ide, 1)
+    V.tensor_scalar(T.wm[0:NR, 0:NR], T.idn[0:NR, 0:NR], 8.0, -0.5, A.mult, A.add).then_inc(S.wk, 1)
 
+    PE.wait_ge(S.ide, 1)
+    PE.wait_ge(S.wk, 4)
+    PE.wait_ge(S.ld, 16)
     for h in (0, 1):
-        V.wait_ge(S["t%d" % h], 1)
-        V.tensor_reduce(T.sums[:, C[h]], pt[h][:, 0:128], X, A.add).then_inc(S["a%d" % h], 1)
-        V.wait_ge(S["a%d" % h], 1)
-        V.tensor_scalar(T.negm[:, C[h]], T.sums[:, C[h]], -cs / 128.0, None, A.mult).then_inc(S["b%d" % h], 1)
-        V.tensor_scalar(T.st[:, C[h]], T.sums[:, C[h]], 1.0 / 8192.0, None, A.mult).then_inc(S["u%d" % h], 1)
-        AC.wait_ge(S["b%d" % h], 1)
-        AC.activation(T.junk[:, H[h]], pt[h][:, 0:128], F.Square, bias=T.negm[:, C[h]], scale=cs,
+        PE.matmul(T.pm[:, C[h]], T.xs[:, H[h]], T.nc[:], True, True).then_inc(S.nn, 1)
+    for h in (0, 1):
+        PE.transpose(pt[h][:, 0:128], T.xs[:, H[h]], T.idn[:]).then_inc(S["t%d" % h], 1)
+    V.wait_ge(S.nn, 2)
+    V.tensor_copy(T.st[:, 0:2], T.pm[:, 0:2]).then_inc(S.ue, 1)
+    AC.wait_ge(S.ue, 1)
+    for h in (0, 1):
+        AC.wait_ge(S["t%d" % h], 1)
+        AC.activation(T.junk[:, H[h]], pt[h][:, 0:128], F.Square, bias=T.st[:, C[h]], scale=1.0 / 32.0,
                       accum_out=T.st[:, 2 + h:3 + h]).then_inc(S["q%d" % h], 1)
 
-    for nm in ("u0", "u1", "q0", "q1"):
+    for nm in ("ue", "q0", "q1"):
         SY.wait_ge(S[nm], 1)
     SY.dma_start(T.dl[rank], T.st[:]).then_inc(S.sd, 16)
 
     AC.wait_ge(S.q0, 1)
     AC.wait_ge(S.q1, 1)
-    AC.activation(T.sdo[:], T.st[:, 2:4], F.Sqrt, bias=EPS).then_inc(S.soe, 1)
+    AC.activation(T.sdo[:], T.st[:, 2:4], F.Sqrt, bias=EPS, scale=0.5).then_inc(S.soe, 1)
     V.wait_ge(S.soe, 1)
     V.reciprocal(T.av[:], T.sdo[:]).then_inc(S.ae, 1)
     V.wait_ge(S.ae, 1)
@@ -112,7 +110,7 @@ def rank_program(g, core, T, topo):
         common &= topo.mask(core, d)
     engines = [1 << i for i in range(16) if (common >> i) & 1]
     left = 0
-    for nm in ("u0", "u1", "q0", "q1"):
+    for nm in ("ue", "q0", "q1"):
         g.wait_ge(S[nm], 1)
     if here:
         g.remote_dma_fused([RemoteDMATransfer(dst_ids=ids_of(here), dma_engine_mask=common, remote_sem=S.arr,
@@ -134,42 +132,46 @@ def rank_program(g, core, T, topo):
     SY.dma_start(T.rk[0:NR, :], T.dl[:]).then_inc(S.rdy, 16)
     PE.wait_ge(S.rdy, 16)
     for h in (0, 1):
-        PE.matmul(pu[h][:, 0:NR], T.rk[0:NR, h:512:4], T.idn[0:NR, 0:NR], True, True).then_inc(S["pu%de" % h], 1)
+        PE.matmul(pu[h][:, 0:NR + 1], T.rk[0:NR, h:512:4], T.wm[0:NR, 0:NR + 1], True, True).then_inc(
+            S["pu%de" % h], 1)
     for h in (0, 1):
-        PE.matmul(T.pq[:, C[h]], T.rk[0:NR, 2 + h:512:4], T.onec[0:NR, :], True, True).then_inc(S.pqe, 1)
+        PE.matmul(T.pq[:, C[h]], T.rk[0:NR, 2 + h:512:4], T.hc[0:NR, :], True, True).then_inc(S.pqe, 1)
 
+    AC.wait_ge(S.a2e, 1)
     for h in (0, 1):
+        AC.wait_ge(S["pu%de" % h], 1)
+        AC.activation(T.junk[:, 256 + 16 * h:272 + 16 * h], pu[h][:, 0:NR], F.Square,
+                      accum_out=T.e2[:, C[h]]).then_inc(S["e%d" % h], 1)
+    for h in (0, 1):
+        AC.wait_ge(S["e%d" % h], 1)
+        AC.wait_ge(S["w%d" % h], 1)
+        AC.activation(T.sdv[:, C[h]], T.e2[:, C[h]], F.Sqrt, bias=T.bb[:, C[h]], scale=T.a2[:, C[h]]).then_inc(S.sq, 1)
+
+    def centre(h):
         V.wait_ge(S["pu%de" % h], 1)
-        V.tensor_reduce(T.negu[:, C[h]], pu[h][:, 0:NR], X, A.add, negate=True).then_inc(S["g%d" % h], 1)
-        AC.wait_ge(S["g%d" % h], 1)
-        AC.activation(T.junk[:, 256 + 16 * h:272 + 16 * h], pu[h][:, 0:NR], F.Square, bias=T.negu[:, C[h]],
-                      scale=16.0, accum_out=T.e2[:, C[h]]).then_inc(S["e%d" % h], 1)
-    V.wait_ge(S.g0, 1)
-    V.wait_ge(S.g1, 1)
-    V.tensor_scalar(T.mu[:], T.negu[:], -4.0, None, A.mult).then_inc(S.mue, 1)
-    V.wait_ge(S.mue, 1)
-    V.wait_ge(S.a2e, 1)
-    for h in (0, 1):
-        V.wait_ge(S["q%d" % h], 1)
-        V.tensor_scalar(T.zc[:, H[h]], pt[h][:, 0:128], T.mu[:, C[h]], T.av[:, C[h]], A.subtract, A.mult).then_inc(
-            S["z%d" % h], 1)
-    V.wait_ge(S.pqe, 2)
-    V.tensor_scalar(T.qe[:], T.pq[:, 0:2], EPS, None, A.add).then_inc(S.qee, 1)
-    V.wait_ge(S.qee, 1)
-    for h in (0, 1):
         V.wait_ge(S["e%d" % h], 1)
-        V.tensor_scalar(T.w[:, C[h]], T.e2[:, C[h]], T.qe[:, C[h]], T.a2[:, C[h]], A.add, A.mult).then_inc(
-            S["w%d" % h], 1)
-    AC.wait_ge(S.w0, 1)
-    AC.wait_ge(S.w1, 1)
-    AC.activation(T.sdv[:], T.w[:], F.Sqrt).then_inc(S.sqe, 1)
-    V.wait_ge(S.sqe, 1)
-    V.reciprocal(T.rr[:], T.sdv[:]).then_inc(S.rce, 1)
-    V.wait_ge(S.rce, 1)
+        V.wait_ge(S["q%d" % h], 1)
+        V.tensor_scalar(T.zc[:, H[h]], pt[h][:, 0:128], pu[h][:, NR:NR + 1], T.av[:, C[h]], A.subtract,
+                        A.mult).then_inc(S["z%d" % h], 1)
+
+    V.wait_ge(S.a2e, 1)
+    centre(0)
+    V.wait_ge(S.pqe, 2)
     for h in (0, 1):
+        V.tensor_scalar(T.bb[:, C[h]], T.pq[:, C[h]], EPS, T.a2[:, C[h]], A.add, A.mult).then_inc(S["w%d" % h], 1)
+    centre(1)
+    V.wait_ge(S.sq, 2)
+    V.reciprocal(T.rr[:], T.sdv[:]).then_inc(S.rc, 1)
+
+    V.wait_ge(S.rc, 1)
+    AC.wait_ge(S.rc, 1)
+    for h in (0, 1):
+        lo, hi = slice(128 * h, 128 * h + 64), slice(128 * h + 64, 128 * h + 128)
         V.wait_ge(S["z%d" % h], 1)
-        V.tensor_scalar(T.yt[:, H[h]], T.zc[:, H[h]], T.rr[:, C[h]], None, A.mult).then_inc(S["y%d" % h], 1)
-        PE.wait_ge(S["y%d" % h], 1)
+        V.tensor_scalar(T.yt[:, lo], T.zc[:, lo], T.rr[:, C[h]], None, A.mult).then_inc(S["y%d" % h], 1)
+        AC.wait_ge(S["z%d" % h], 1)
+        AC.activation(T.yt[:, hi], T.zc[:, hi], F.Identity, scale=T.rr[:, C[h]]).then_inc(S["y%d" % h], 1)
+        PE.wait_ge(S["y%d" % h], 2)
         PE.transpose(py[h][:, 0:128], T.yt[:, H[h]], T.idn[:]).then_inc(S["py%de" % h], 1)
 
     AC.wait_ge(S.py0e, 1)

@@ -3,11 +3,13 @@ from concourse.mybir import AluOpType, ActivationFunctionType
 
 NR = 16
 EPS = 0.01
+REPS = 0.025
 
 SCRATCH = {
     "xs": ("sbuf", [128, 256], "float32"),
+    "pmi": ("sbuf", [128, 128], "float32"),
     "idn": ("sbuf", [128, 128], "float32"),
-    "nc": ("sbuf", [128, 1], "float32"),
+    "cm": ("sbuf", [128, 129], "float32"),
     "hc": ("sbuf", [128, 1], "float32"),
     "wm": ("sbuf", [128, 20], "float32"),
     "st": ("sbuf", [128, 4], "float32"),
@@ -17,25 +19,25 @@ SCRATCH = {
     "sdo": ("sbuf", [128, 2], "float32"),
     "av": ("sbuf", [128, 2], "float32"),
     "a2": ("sbuf", [128, 2], "float32"),
+    "ab": ("sbuf", [128, 2], "float32"),
     "e2": ("sbuf", [128, 2], "float32"),
-    "bb": ("sbuf", [128, 2], "float32"),
     "sdv": ("sbuf", [128, 2], "float32"),
     "rr": ("sbuf", [128, 2], "float32"),
     "zc": ("sbuf", [128, 256], "float32"),
     "yt": ("sbuf", [128, 256], "float32"),
     "ys": ("sbuf", [128, 256], "float32"),
-    "pm": ("psum", [128, 512], "float32"),
     "pt0": ("psum", [128, 512], "float32"),
     "pt1": ("psum", [128, 512], "float32"),
     "py0": ("psum", [128, 512], "float32"),
     "py1": ("psum", [128, 512], "float32"),
+    "py2": ("psum", [128, 512], "float32"),
     "pu0": ("psum", [128, 512], "float32"),
     "pu1": ("psum", [128, 512], "float32"),
     "pq": ("psum", [128, 512], "float32"),
 }
-SEMAPHORES = ["ld", "m1", "wk", "ide", "nn", "t0", "t1", "ue", "q0", "q1", "sd", "arr", "loc", "rdy", "pu0e", "pu1e",
-              "pqe", "e0", "e1", "w0", "w1", "z0", "z1", "sq", "rc", "soe", "ae", "a2e", "y0", "y1", "py0e", "py1e",
-              "c0", "c1", "s0", "s1"]
+SEMAPHORES = ["ld", "ioe", "wk", "ide", "wc", "t0", "t1", "q0", "q1", "sd", "arr", "loc", "rdy", "pu0e", "pu1e",
+              "pq0e", "pq1e", "e0", "e1", "x0", "x1", "z0", "z1", "sq", "rc", "soe", "ae", "a2e", "y0", "y1",
+              "py0e", "py1e", "py2e", "c0", "c1", "s0", "s1"]
 
 
 def rank_program(g, core, T, topo):
@@ -47,47 +49,48 @@ def rank_program(g, core, T, topo):
     F = ActivationFunctionType
     V, AC, PE, SY = g.vector, g.scalar, g.tensor, g.sync
     pt = [T.pt0, T.pt1]
-    py = [T.py0, T.py1]
     pu = [T.pu0, T.pu1]
+    pqc = [T.pq[:, 0:1], T.py2[:, 256:257]]
     H = [slice(0, 128), slice(128, 256)]
     C = [slice(0, 1), slice(1, 2)]
 
     SY.dma_start(T.xs[:], T.x[:]).then_inc(S.ld, 16)
-    V.memset(T.idn[:], 1.0).then_inc(S.m1, 1)
-    g.wait_ge(S.m1, 1)
-    g.affine_select(T.idn[:], T.idn[:], [[-1, 128]], A.is_equal, 0.0, 0, 1).then_inc(S.ide, 1)
-    V.memset(T.nc[:], -1.0 / 4096.0).then_inc(S.wk, 1)
-    V.memset(T.hc[:], 0.5).then_inc(S.wk, 1)
-    V.memset(T.wm[0:NR, NR:NR + 1], -2.0).then_inc(S.wk, 1)
+    g.iota(T.pmi[:], [[-1, 128]], 0, 1, allow_small_or_imprecise_dtypes=True).then_inc(S.ioe, 1)
+    V.memset(T.cm[:, 128:129], -1.0 / 4096.0).then_inc(S.wk, 1)
+    V.wait_ge(S.ioe, 1)
+    V.tensor_scalar(T.cm[:, 0:128], T.pmi[:], 0.0, -1.0 / 128.0, A.is_equal, A.add).then_inc(S.wk, 1)
+    V.tensor_scalar(T.idn[:], T.pmi[:], 0.0, None, A.is_equal).then_inc(S.ide, 1)
+    V.memset(T.hc[:], 0.5).then_inc(S.wc, 1)
+    V.memset(T.wm[0:NR, NR:NR + 1], -2.0).then_inc(S.wc, 1)
     V.wait_ge(S.ide, 1)
-    V.tensor_scalar(T.wm[0:NR, 0:NR], T.idn[0:NR, 0:NR], 8.0, -0.5, A.mult, A.add).then_inc(S.wk, 1)
+    V.tensor_scalar(T.wm[0:NR, 0:NR], T.idn[0:NR, 0:NR], 8.0, -0.5, A.mult, A.add).then_inc(S.wc, 1)
 
-    PE.wait_ge(S.ide, 1)
-    PE.wait_ge(S.wk, 4)
+    PE.wait_ge(S.wk, 2)
     PE.wait_ge(S.ld, 16)
     for h in (0, 1):
-        PE.matmul(T.pm[:, C[h]], T.xs[:, H[h]], T.nc[:], True, True).then_inc(S.nn, 1)
-    for h in (0, 1):
-        PE.transpose(pt[h][:, 0:128], T.xs[:, H[h]], T.idn[:]).then_inc(S["t%d" % h], 1)
-    V.wait_ge(S.nn, 2)
-    V.tensor_copy(T.st[:, 0:2], T.pm[:, 0:2]).then_inc(S.ue, 1)
-    AC.wait_ge(S.ue, 1)
+        PE.matmul(pt[h][:, 0:129], T.xs[:, H[h]], T.cm[:, 0:129], True, True).then_inc(S["t%d" % h], 1)
     for h in (0, 1):
         AC.wait_ge(S["t%d" % h], 1)
-        AC.activation(T.junk[:, H[h]], pt[h][:, 0:128], F.Square, bias=T.st[:, C[h]], scale=1.0 / 32.0,
+        AC.activation(T.junk[:, H[h]], pt[h][:, 0:128], F.Square, scale=1.0 / 32.0,
                       accum_out=T.st[:, 2 + h:3 + h]).then_inc(S["q%d" % h], 1)
+        AC.activation(T.st[:, C[h]], pt[h][:, 128:129], F.Copy).then_inc(S["q%d" % h], 1)
 
-    for nm in ("ue", "q0", "q1"):
-        SY.wait_ge(S[nm], 1)
+    for nm in ("q0", "q1"):
+        SY.wait_ge(S[nm], 2)
     SY.dma_start(T.dl[rank], T.st[:]).then_inc(S.sd, 16)
 
-    AC.wait_ge(S.q0, 1)
-    AC.wait_ge(S.q1, 1)
+    AC.wait_ge(S.q0, 2)
+    AC.wait_ge(S.q1, 2)
     AC.activation(T.sdo[:], T.st[:, 2:4], F.Sqrt, bias=EPS, scale=0.5).then_inc(S.soe, 1)
     V.wait_ge(S.soe, 1)
     V.reciprocal(T.av[:], T.sdo[:]).then_inc(S.ae, 1)
     V.wait_ge(S.ae, 1)
     V.tensor_tensor(T.a2[:], T.av[:], T.av[:], A.mult).then_inc(S.a2e, 1)
+    V.tensor_scalar(T.ab[:], T.av[:], REPS, None, A.mult).then_inc(S.a2e, 1)
+    PE.wait_ge(S.ide, 1)
+    for h in (0, 1):
+        PE.wait_ge(S["q%d" % h], 2)
+        PE.transpose(pt[h][:, 0:128], T.xs[:, H[h]], T.idn[:]).then_inc(S["x%d" % h], 1)
 
     def far(d):
         a, b = topo.chip(core), topo.chip(d)
@@ -110,8 +113,8 @@ def rank_program(g, core, T, topo):
         common &= topo.mask(core, d)
     engines = [1 << i for i in range(16) if (common >> i) & 1]
     left = 0
-    for nm in ("ue", "q0", "q1"):
-        g.wait_ge(S[nm], 1)
+    for nm in ("q0", "q1"):
+        g.wait_ge(S[nm], 2)
     if here:
         g.remote_dma_fused([RemoteDMATransfer(dst_ids=ids_of(here), dma_engine_mask=common, remote_sem=S.arr,
                                               srcs=[T.st[:]], dsts=[T.dl[rank] for _ in here], alu_op=0)],
@@ -130,36 +133,30 @@ def rank_program(g, core, T, topo):
     SY.wait_ge(S.sd, 16)
     SY.wait_ge(S.arr, len(here) * len(engines) + len(away))
     SY.dma_start(T.rk[0:NR, :], T.dl[:]).then_inc(S.rdy, 16)
+    PE.wait_ge(S.wc, 3)
     PE.wait_ge(S.rdy, 16)
     for h in (0, 1):
         PE.matmul(pu[h][:, 0:NR + 1], T.rk[0:NR, h:512:4], T.wm[0:NR, 0:NR + 1], True, True).then_inc(
             S["pu%de" % h], 1)
     for h in (0, 1):
-        PE.matmul(T.pq[:, C[h]], T.rk[0:NR, 2 + h:512:4], T.hc[0:NR, :], True, True).then_inc(S.pqe, 1)
+        PE.matmul(pqc[h], T.rk[0:NR, 2 + h:512:4], T.hc[0:NR, :], True, True).then_inc(S["pq%de" % h], 1)
 
-    AC.wait_ge(S.a2e, 1)
+    AC.wait_ge(S.a2e, 2)
     for h in (0, 1):
         AC.wait_ge(S["pu%de" % h], 1)
-        AC.activation(T.junk[:, 256 + 16 * h:272 + 16 * h], pu[h][:, 0:NR], F.Square,
-                      accum_out=T.e2[:, C[h]]).then_inc(S["e%d" % h], 1)
+        AC.activation(T.junk[:, 256 + 16 * h:272 + 16 * h], pu[h][:, 0:NR], F.Square, bias=T.ab[:, C[h]],
+                      scale=T.av[:, C[h]], accum_out=T.e2[:, C[h]]).then_inc(S["e%d" % h], 1)
     for h in (0, 1):
         AC.wait_ge(S["e%d" % h], 1)
-        AC.wait_ge(S["w%d" % h], 1)
-        AC.activation(T.sdv[:, C[h]], T.e2[:, C[h]], F.Sqrt, bias=T.bb[:, C[h]], scale=T.a2[:, C[h]]).then_inc(S.sq, 1)
+        AC.wait_ge(S["pq%de" % h], 1)
+        AC.activation(T.sdv[:, C[h]], pqc[h], F.Sqrt, bias=T.e2[:, C[h]], scale=T.a2[:, C[h]]).then_inc(S.sq, 1)
 
-    def centre(h):
+    for h in (0, 1):
+        V.wait_ge(S["x%d" % h], 1)
         V.wait_ge(S["pu%de" % h], 1)
         V.wait_ge(S["e%d" % h], 1)
-        V.wait_ge(S["q%d" % h], 1)
         V.tensor_scalar(T.zc[:, H[h]], pt[h][:, 0:128], pu[h][:, NR:NR + 1], T.av[:, C[h]], A.subtract,
                         A.mult).then_inc(S["z%d" % h], 1)
-
-    V.wait_ge(S.a2e, 1)
-    centre(0)
-    V.wait_ge(S.pqe, 2)
-    for h in (0, 1):
-        V.tensor_scalar(T.bb[:, C[h]], T.pq[:, C[h]], EPS, T.a2[:, C[h]], A.add, A.mult).then_inc(S["w%d" % h], 1)
-    centre(1)
     V.wait_ge(S.sq, 2)
     V.reciprocal(T.rr[:], T.sdv[:]).then_inc(S.rc, 1)
 
@@ -171,16 +168,21 @@ def rank_program(g, core, T, topo):
         V.tensor_scalar(T.yt[:, lo], T.zc[:, lo], T.rr[:, C[h]], None, A.mult).then_inc(S["y%d" % h], 1)
         AC.wait_ge(S["z%d" % h], 1)
         AC.activation(T.yt[:, hi], T.zc[:, hi], F.Identity, scale=T.rr[:, C[h]]).then_inc(S["y%d" % h], 1)
-        PE.wait_ge(S["y%d" % h], 2)
-        PE.transpose(py[h][:, 0:128], T.yt[:, H[h]], T.idn[:]).then_inc(S["py%de" % h], 1)
+    PE.wait_ge(S.y0, 2)
+    PE.transpose(T.py0[:, 0:128], T.yt[:, H[0]], T.idn[:]).then_inc(S.py0e, 1)
+    PE.wait_ge(S.y1, 2)
+    PE.matmul(T.py1[:, 0:64], T.yt[0:64, H[1]], T.idn[0:64, 0:64], True, True).then_inc(S.py1e, 1)
+    PE.matmul(T.py2[:, 0:64], T.yt[64:128, H[1]], T.idn[64:128, 64:128], True, True).then_inc(S.py2e, 1)
 
     AC.wait_ge(S.py0e, 1)
-    AC.activation(T.ys[:, H[0]], py[0][:, 0:128], F.Copy).then_inc(S.c0, 1)
+    AC.activation(T.ys[:, H[0]], T.py0[:, 0:128], F.Copy).then_inc(S.c0, 1)
     AC.wait_ge(S.c0, 1)
     AC.dma_start(T.y[:, H[0]], T.ys[:, H[0]]).then_inc(S.s0, 16)
     V.wait_ge(S.py1e, 1)
-    V.tensor_copy(T.ys[:, H[1]], py[1][:, 0:128]).then_inc(S.c1, 1)
-    SY.wait_ge(S.c1, 1)
+    V.tensor_copy(T.ys[:, 128:192], T.py1[:, 0:64]).then_inc(S.c1, 1)
+    V.wait_ge(S.py2e, 1)
+    V.tensor_copy(T.ys[:, 192:256], T.py2[:, 0:64]).then_inc(S.c1, 1)
+    SY.wait_ge(S.c1, 2)
     SY.dma_start(T.y[:, H[1]], T.ys[:, H[1]]).then_inc(S.s1, 16)
 
     g.wait_ge(S.loc, left)

from concourse.bass import DstId, RemoteDMATransfer
from concourse.mybir import AluOpType, ActivationFunctionType

NR = 16
EPS = 0.01
REPS = 0.025

SCRATCH = {
    "xs": ("sbuf", [128, 256], "float32"),
    "pmi": ("sbuf", [128, 128], "float32"),
    "idn": ("sbuf", [128, 128], "float32"),
    "cm": ("sbuf", [128, 129], "float32"),
    "hc": ("sbuf", [128, 1], "float32"),
    "wm": ("sbuf", [128, 20], "float32"),
    "st": ("sbuf", [128, 4], "float32"),
    "junk": ("sbuf", [128, 288], "float32"),
    "dl": ("dram", [NR, 128, 4], "float32"),
    "rk": ("sbuf", [128, 512], "float32"),
    "sdo": ("sbuf", [128, 2], "float32"),
    "av": ("sbuf", [128, 2], "float32"),
    "a2": ("sbuf", [128, 2], "float32"),
    "ab": ("sbuf", [128, 2], "float32"),
    "e2": ("sbuf", [128, 2], "float32"),
    "sdv": ("sbuf", [128, 2], "float32"),
    "rr": ("sbuf", [128, 2], "float32"),
    "zc": ("sbuf", [128, 256], "float32"),
    "yt": ("sbuf", [128, 256], "float32"),
    "ys": ("sbuf", [128, 256], "float32"),
    "pt0": ("psum", [128, 512], "float32"),
    "pt1": ("psum", [128, 512], "float32"),
    "py0": ("psum", [128, 512], "float32"),
    "py1": ("psum", [128, 512], "float32"),
    "py2": ("psum", [128, 512], "float32"),
    "pu0": ("psum", [128, 512], "float32"),
    "pu1": ("psum", [128, 512], "float32"),
    "pq": ("psum", [128, 512], "float32"),
}
SEMAPHORES = ["ld", "ioe", "wk", "ide", "wc", "t0", "t1", "q0", "q1", "sd", "arr", "loc", "rdy", "pu0e", "pu1e",
              "pq0e", "pq1e", "e0", "e1", "x0", "x1", "z0", "z1", "sq", "rc", "soe", "ae", "a2e", "y0", "y1",
              "py0e", "py1e", "py2e", "c0", "c1", "s0", "s1"]


def rank_program(g, core, T, topo):
    rank = T.rank_of(core)
    if rank is None:
        return
    S = T.sem
    A = AluOpType
    F = ActivationFunctionType
    V, AC, PE, SY = g.vector, g.scalar, g.tensor, g.sync
    pt = [T.pt0, T.pt1]
    pu = [T.pu0, T.pu1]
    pqc = [T.pq[:, 0:1], T.py2[:, 256:257]]
    H = [slice(0, 128), slice(128, 256)]
    C = [slice(0, 1), slice(1, 2)]

    SY.dma_start(T.xs[:], T.x[:]).then_inc(S.ld, 16)
    g.iota(T.pmi[:], [[-1, 128]], 0, 1, allow_small_or_imprecise_dtypes=True).then_inc(S.ioe, 1)
    V.memset(T.cm[:, 128:129], -1.0 / 4096.0).then_inc(S.wk, 1)
    V.wait_ge(S.ioe, 1)
    V.tensor_scalar(T.cm[:, 0:128], T.pmi[:], 0.0, -1.0 / 128.0, A.is_equal, A.add).then_inc(S.wk, 1)
    V.tensor_scalar(T.idn[:], T.pmi[:], 0.0, None, A.is_equal).then_inc(S.ide, 1)
    V.memset(T.hc[:], 0.5).then_inc(S.wc, 1)
    V.memset(T.wm[0:NR, NR:NR + 1], -2.0).then_inc(S.wc, 1)
    V.wait_ge(S.ide, 1)
    V.tensor_scalar(T.wm[0:NR, 0:NR], T.idn[0:NR, 0:NR], 8.0, -0.5, A.mult, A.add).then_inc(S.wc, 1)

    PE.wait_ge(S.wk, 2)
    PE.wait_ge(S.ld, 16)
    for h in (0, 1):
        PE.matmul(pt[h][:, 0:129], T.xs[:, H[h]], T.cm[:, 0:129], True, True).then_inc(S["t%d" % h], 1)
    for h in (0, 1):
        AC.wait_ge(S["t%d" % h], 1)
        AC.activation(T.junk[:, H[h]], pt[h][:, 0:128], F.Square, scale=1.0 / 32.0,
                      accum_out=T.st[:, 2 + h:3 + h]).then_inc(S["q%d" % h], 1)
        AC.activation(T.st[:, C[h]], pt[h][:, 128:129], F.Copy).then_inc(S["q%d" % h], 1)

    for nm in ("q0", "q1"):
        SY.wait_ge(S[nm], 2)
    SY.dma_start(T.dl[rank], T.st[:]).then_inc(S.sd, 16)

    AC.wait_ge(S.q0, 2)
    AC.wait_ge(S.q1, 2)
    AC.activation(T.sdo[:], T.st[:, 2:4], F.Sqrt, bias=EPS, scale=0.5).then_inc(S.soe, 1)
    V.wait_ge(S.soe, 1)
    V.reciprocal(T.av[:], T.sdo[:]).then_inc(S.ae, 1)
    V.wait_ge(S.ae, 1)
    V.tensor_tensor(T.a2[:], T.av[:], T.av[:], A.mult).then_inc(S.a2e, 1)
    V.tensor_scalar(T.ab[:], T.av[:], REPS, None, A.mult).then_inc(S.a2e, 1)
    PE.wait_ge(S.ide, 1)
    for h in (0, 1):
        PE.wait_ge(S["q%d" % h], 2)
        PE.transpose(pt[h][:, 0:128], T.xs[:, H[h]], T.idn[:]).then_inc(S["x%d" % h], 1)

    def far(d):
        a, b = topo.chip(core), topo.chip(d)
        if a == b:
            return 0
        return 1 if (topo.mates(a, b) or topo.same_plane(a, b)) else 2

    def ids_of(ds):
        out = []
        for d in ds:
            rid, pid, _ = topo.addr(d)
            out.append(DstId(rid=rid, pnc=pid))
        return out

    others = [d for d in T.cores if d != core and topo.may_write(core, d)]
    here = [d for d in others if far(d) == 0]
    away = sorted([d for d in others if far(d) > 0], key=lambda d: -far(d))
    common = 0xFFFF
    for d in others:
        common &= topo.mask(core, d)
    engines = [1 << i for i in range(16) if (common >> i) & 1]
    left = 0
    for nm in ("q0", "q1"):
        g.wait_ge(S[nm], 2)
    if here:
        g.remote_dma_fused([RemoteDMATransfer(dst_ids=ids_of(here), dma_engine_mask=common, remote_sem=S.arr,
                                              srcs=[T.st[:]], dsts=[T.dl[rank] for _ in here], alu_op=0)],
                           local_sem=S.loc)
        left += len(engines)
    transfers = []
    for i, e in enumerate(engines):
        ds = away[i::len(engines)]
        if ds:
            transfers.append(RemoteDMATransfer(dst_ids=ids_of(ds), dma_engine_mask=e, remote_sem=S.arr,
                                               srcs=[T.dl[rank]], dsts=[T.dl[rank] for _ in ds], alu_op=0))
    g.wait_ge(S.sd, 16)
    g.remote_dma_fused(transfers, local_sem=S.loc)
    left += len(transfers)

    SY.wait_ge(S.sd, 16)
    SY.wait_ge(S.arr, len(here) * len(engines) + len(away))
    SY.dma_start(T.rk[0:NR, :], T.dl[:]).then_inc(S.rdy, 16)
    PE.wait_ge(S.wc, 3)
    PE.wait_ge(S.rdy, 16)
    for h in (0, 1):
        PE.matmul(pu[h][:, 0:NR + 1], T.rk[0:NR, h:512:4], T.wm[0:NR, 0:NR + 1], True, True).then_inc(
            S["pu%de" % h], 1)
    for h in (0, 1):
        PE.matmul(pqc[h], T.rk[0:NR, 2 + h:512:4], T.hc[0:NR, :], True, True).then_inc(S["pq%de" % h], 1)

    AC.wait_ge(S.a2e, 2)
    for h in (0, 1):
        AC.wait_ge(S["pu%de" % h], 1)
        AC.activation(T.junk[:, 256 + 16 * h:272 + 16 * h], pu[h][:, 0:NR], F.Square, bias=T.ab[:, C[h]],
                      scale=T.av[:, C[h]], accum_out=T.e2[:, C[h]]).then_inc(S["e%d" % h], 1)
    for h in (0, 1):
        AC.wait_ge(S["e%d" % h], 1)
        AC.wait_ge(S["pq%de" % h], 1)
        AC.activation(T.sdv[:, C[h]], pqc[h], F.Sqrt, bias=T.e2[:, C[h]], scale=T.a2[:, C[h]]).then_inc(S.sq, 1)

    for h in (0, 1):
        V.wait_ge(S["x%d" % h], 1)
        V.wait_ge(S["pu%de" % h], 1)
        V.wait_ge(S["e%d" % h], 1)
        V.tensor_scalar(T.zc[:, H[h]], pt[h][:, 0:128], pu[h][:, NR:NR + 1], T.av[:, C[h]], A.subtract,
                        A.mult).then_inc(S["z%d" % h], 1)
    V.wait_ge(S.sq, 2)
    V.reciprocal(T.rr[:], T.sdv[:]).then_inc(S.rc, 1)

    V.wait_ge(S.rc, 1)
    AC.wait_ge(S.rc, 1)
    for h in (0, 1):
        lo, hi = slice(128 * h, 128 * h + 64), slice(128 * h + 64, 128 * h + 128)
        V.wait_ge(S["z%d" % h], 1)
        V.tensor_scalar(T.yt[:, lo], T.zc[:, lo], T.rr[:, C[h]], None, A.mult).then_inc(S["y%d" % h], 1)
        AC.wait_ge(S["z%d" % h], 1)
        AC.activation(T.yt[:, hi], T.zc[:, hi], F.Identity, scale=T.rr[:, C[h]]).then_inc(S["y%d" % h], 1)
    PE.wait_ge(S.y0, 2)
    PE.transpose(T.py0[:, 0:128], T.yt[:, H[0]], T.idn[:]).then_inc(S.py0e, 1)
    PE.wait_ge(S.y1, 2)
    PE.matmul(T.py1[:, 0:64], T.yt[0:64, H[1]], T.idn[0:64, 0:64], True, True).then_inc(S.py1e, 1)
    PE.matmul(T.py2[:, 0:64], T.yt[64:128, H[1]], T.idn[64:128, 64:128], True, True).then_inc(S.py2e, 1)

    AC.wait_ge(S.py0e, 1)
    AC.activation(T.ys[:, H[0]], T.py0[:, 0:128], F.Copy).then_inc(S.c0, 1)
    AC.wait_ge(S.c0, 1)
    AC.dma_start(T.y[:, H[0]], T.ys[:, H[0]]).then_inc(S.s0, 16)
    V.wait_ge(S.py1e, 1)
    V.tensor_copy(T.ys[:, 128:192], T.py1[:, 0:64]).then_inc(S.c1, 1)
    V.wait_ge(S.py2e, 1)
    V.tensor_copy(T.ys[:, 192:256], T.py2[:, 0:64]).then_inc(S.c1, 1)
    SY.wait_ge(S.c1, 2)
    SY.dma_start(T.y[:, H[1]], T.ys[:, H[1]]).then_inc(S.s1, 16)

    g.wait_ge(S.loc, left)
    AC.wait_ge(S.s0, 16)
    SY.wait_ge(S.s1, 16)
